import numpy as np
import ml_dtypes


def mxq(x, axis, fmt="e4m3"):
    dtype, down = {"e4m3": (ml_dtypes.float8_e4m3fn, 7), "e5m2": (ml_dtypes.float8_e5m2, 14)}[fmt]
    v = np.moveaxis(np.asarray(x, np.float32).astype(ml_dtypes.bfloat16).astype(np.float64), axis, -1)
    blocks = v.reshape(v.shape[:-1] + (-1, 32))
    amax = np.abs(blocks).max(-1, keepdims=True)
    byte = np.maximum(np.where(amax > 0, np.frexp(amax)[1] - 1 + 127, 0) - down, 1)
    scale = np.exp2(byte - 127.0)
    codes = (blocks / scale).astype(np.float32).astype(dtype).astype(np.float64)
    return np.moveaxis((codes * scale).reshape(v.shape), -1, axis)


WIDE = False


def mx_kscale(k):
    if not WIDE:
        return np.ones(k)
    levels = np.array([30, -30])
    if k % 512:
        return np.exp2(np.random.permutation(np.resize(levels, k // 32))).repeat(32)
    a = np.empty((k // 512, 16))
    for p in range(k // 512):
        a[p, :8] = np.random.permutation(np.resize(levels, 8))
        for g in range(8):
            far = levels[np.abs(levels - a[p, g]) >= 10]
            a[p, g + 8] = far[np.random.randint(len(far))]
    return np.exp2(a.ravel()).repeat(32)


def f64(x):
    return np.asarray(x).astype(np.float64)


def striped(idx):
    return np.tile(np.asarray(idx).reshape(-1, 16).T, (8, 1)).astype(np.uint16)


def unstriped(offs):
    return offs[:16].T.reshape(-1).astype(np.int64)


E2M1 = np.array([0.0, 0.5, 1.0, 1.5, 2.0, 3.0, 4.0, 6.0, -0.0, -0.5, -1.0, -1.5, -2.0, -3.0, -4.0, -6.0])


def pack_weight(w, fmt):
    k, n = w.shape
    w = f64(np.asarray(w, np.float32).astype(ml_dtypes.bfloat16)).reshape(k // 32, 32, n)
    amax = np.abs(w).max(1)
    if fmt in ("e4m3", "e5m2"):
        byte = np.frexp(amax)[1] - 1 + 127 - (7 if fmt == "e4m3" else 14)
    else:
        mant, ex = np.frexp(amax / 6.0)
        byte = np.where(mant > 0.5, ex, ex - 1) + 127
    byte = np.clip(np.where(amax > 0, byte, 1), 1, 254)
    scaled = (w * np.exp2(127.0 - byte)[:, None, :]).reshape(k, n).astype(np.float32)
    by_word = np.ascontiguousarray(scaled.reshape(k // 512, 128, 4, n).transpose(0, 1, 3, 2))
    if fmt in ("e4m3", "e5m2"):
        words = by_word.astype(ml_dtypes.float8_e4m3fn if fmt == "e4m3" else ml_dtypes.float8_e5m2).view(np.uint8)
    else:
        c = by_word.astype(ml_dtypes.float4_e2m1fn).view(np.uint8) & 0xF
        words = (c[..., 0::2] | (c[..., 1::2] << 4)).reshape(k // 512, 128, 2 * n)
    return np.ascontiguousarray(words), np.ascontiguousarray(byte.astype(np.uint8).reshape(k // 512, 16, n))


def unpack_weight(words, scales, fmt):
    g, _, n = scales.shape
    words = np.ascontiguousarray(words).reshape(g, 128, n, -1)
    if fmt in ("e4m3", "e5m2"):
        vals = words.view(ml_dtypes.float8_e4m3fn if fmt == "e4m3" else ml_dtypes.float8_e5m2).astype(np.float64)
    else:
        nib = np.empty((g, 128, n, 4), np.uint8)
        nib[..., 0::2] = words & 0xF
        nib[..., 1::2] = words >> 4
        vals = E2M1[nib]
    vals = vals * np.repeat(np.exp2(scales.astype(np.float64) - 127.0), 8, axis=1)[..., None]
    return vals.transpose(0, 1, 3, 2).reshape(g * 512, n)


K, T, J, R, C, N, E = 512, 2048, 256, 512, 512, 256, 1024


def setup_inputs():
    n = np.random.standard_normal
    idx = np.random.permutation(T)[:J]
    idx2 = np.random.permutation(T)[:J]
    idx3 = np.random.permutation(C)[:J]
    idx4 = np.random.permutation(C)[:J]
    idx5 = np.random.permutation(E)[:J]
    fk = mx_kscale(K)
    fr = mx_kscale(R)
    xtp = pack_weight(n((K, T)) / fk[:, None], "e2m1")
    wp = pack_weight(n((K, R)) * 1 / np.sqrt(K) * fk[:, None] * fr, "e5m2")
    wbp = pack_weight(n((R, N)) * 1 / np.sqrt(R) / fr[:, None], "e4m3")
    wsp = pack_weight(n((K, N)) * 1 / np.sqrt(K) * fk[:, None], "e4m3")
    return {
        "xt_words": xtp[0],
        "xt_scales": xtp[1],
        "w_words": wp[0],
        "w_scales": wp[1],
        "wb_words": wbp[0],
        "wb_scales": wbp[1],
        "ws_words": wsp[0],
        "ws_scales": wsp[1],
        "offs": striped(idx),
        "offs2": striped(idx2),
        "offs3": striped(idx3),
        "offs4": striped(idx4),
        "offs5": striped(idx5),
    }


def reference(xt_words, xt_scales, w_words, w_scales, wb_words, wb_scales, ws_words, ws_scales, offs, offs2, offs3, offs4, offs5):
    idx = unstriped(offs)
    idx2 = unstriped(offs2)
    idx3 = unstriped(offs3)
    idx4 = unstriped(offs4)
    idx5 = unstriped(offs5)
    xtu = unpack_weight(xt_words, xt_scales, "e2m1")
    wu = unpack_weight(w_words, w_scales, "e5m2")
    wbu = unpack_weight(wb_words, wb_scales, "e4m3")
    wsu = unpack_weight(ws_words, ws_scales, "e4m3")
    xtidxg = xtu[:, idx]
    a = wu.T @ xtidxg
    xtidx2g = xtu[:, idx2]
    b = wu.T @ xtidx2g
    pw = np.zeros((R, C))
    pw[:, idx3] = a
    hid = np.maximum(pw[:, idx4], b)
    hidq = mxq(hid, 0, "e5m2")
    p = wbu.T @ hidq + wsu.T @ xtidxg
    y = np.zeros((N, E))
    y[:, idx5] = p
    return y

@@ -1,0 +1,224 @@
+from contextlib import ExitStack
+
+import concourse.mybir as mybir
+
+K, T, J, R, C, N, E = 512, 2048, 256, 512, 512, 256, 1024
+FLOPS = 2 * K * R * J * 2 + 2 * R * N * J + 2 * K * N * J
+
+F32 = mybir.dt.float32
+BF16 = mybir.dt.bfloat16
+I32 = mybir.dt.int32
+U32 = mybir.dt.uint32
+U16 = mybir.dt.uint16
+U8 = mybir.dt.uint8
+E4M3 = mybir.dt.float8_e4m3fn_x4
+E5M2 = mybir.dt.float8_e5m2_x4
+E2M1 = mybir.dt.float4_e2m1fn_x4
+COPY = mybir.ActivationFunctionType.Copy
+MAX = mybir.AluOpType.max
+
+P = 128
+PACK = 4
+HALF = J // 2
+HALF_COLS = HALF // 16
+SPLIT = 192
+
+
+def load_words(nc, tile, words):
+    nc.sync.dma_start(out=tile[:].bitcast(I32), in_=words.bitcast(I32))
+
+
+def load_scale_rows(queue, plane, scales):
+    for q in range(4):
+        queue.dma_start(
+            out=plane[32 * q : 32 * q + 4, :].bitcast(I32),
+            in_=scales[0, 4 * q : 4 * q + 4, :].bitcast(I32),
+        )
+
+
+def move(nc, on_scalar, out, in_):
+    if on_scalar:
+        nc.scalar.activation(out=out, in_=in_, func=COPY)
+    else:
+        nc.vector.tensor_copy(out=out, in_=in_)
+
+
+def tile_list_tied_board_skip_scattered_kernel(
+    tc, xt_words, xt_scales, w_words, w_scales, wb_words, wb_scales, ws_words, ws_scales,
+    offs, offs2, offs3, offs4, offs5, out,
+):
+    nc = tc.nc
+    with ExitStack() as ctx:
+        lists = ctx.enter_context(tc.tile_pool(name="lists", bufs=1))
+        sb = ctx.enter_context(tc.tile_pool(name="sb", bufs=1))
+        stage = ctx.enter_context(tc.tile_pool(name="stage", bufs=1))
+        psum = ctx.enter_context(tc.psum_pool(name="psum", bufs=1))
+
+        first_list = lists.tile([P, J // 16], U16, name="first_list")
+        second_list = lists.tile([P, J // 16], U16, name="second_list")
+        put_list = lists.tile([P, J // 16], U16, name="put_list")
+        read_list = lists.tile([P, J // 16], U16, name="read_list")
+        page_list = lists.tile([P, J // 16], U16, name="page_list")
+
+        xt_codes = sb.tile([P, T], U16, name="xt_codes", tag="xt_codes", align_bytes=64)
+        xt_plane = sb.tile([P, T], U8, name="xt_plane", tag="xt_plane", align_bytes=64)
+        w_codes_in = sb.tile([P, R], U32, name="w_codes_in", tag="w_codes_in", align_bytes=64)
+        w_plane_in = sb.tile([P, R], U8, name="w_plane_in", tag="w_plane_in", align_bytes=64)
+        ws_plane = sb.tile([P, N], U8, name="ws_plane", align_bytes=64)
+        wb_plane = sb.tile([P, N], U8, name="wb_plane", align_bytes=64)
+        boards = [sb.tile([P, C], F32, name=f"board{t}") for t in range(PACK)]
+
+        nc.vector.memset(xt_plane[:].bitcast(I32), 0)
+        nc.gpsimd.memset(w_plane_in[:].bitcast(I32), 0)
+
+        nc.sync.dma_start(first_list[:], offs)
+        nc.sync.dma_start(second_list[:], offs2)
+        nc.sync.dma_start(put_list[:], offs3)
+        load_scale_rows(nc.sync, xt_plane, xt_scales)
+        load_words(nc, xt_codes, xt_words[0])
+        load_words(nc, w_codes_in, w_words[0].rearrange("p n t -> p (n t)"))
+        load_scale_rows(nc.sync, w_plane_in, w_scales)
+
+        for t in range(PACK):
+            nc.gpsimd.memset(boards[t][:], 0.0)
+        nc.vector.memset(ws_plane[:].bitcast(I32), 0)
+        nc.vector.memset(wb_plane[:].bitcast(I32), 0)
+
+        nc.sync.dma_start(read_list[:], offs4)
+        nc.sync.dma_start(page_list[:], offs5)
+        load_scale_rows(nc.sync, ws_plane, ws_scales)
+        load_scale_rows(nc.sync, wb_plane, wb_scales)
+
+        x1_plane = sb.tile([P, J], U8, name="x1_plane", align_bytes=64)
+        x1_codes = sb.tile([P, J], U16, name="x1_codes", align_bytes=64)
+        x2_plane = sb.tile([P, J], U8, name="x2_plane", align_bytes=64)
+        nc.vector.tensor_copy(out=x1_plane[:], in_=xt_plane[:].indirect(first_list[:]))
+        nc.vector.tensor_copy(out=x1_codes[:], in_=xt_codes[:].indirect(first_list[:]))
+
+        w_pairs = []
+        for u in range(2):
+            w_pair = sb.tile([P, 2, P], U32, name=f"w_pair{u}", align_bytes=64)
+            nc.scalar.copy(
+                out=w_pair[:].rearrange("p t m -> p m t"),
+                in_=w_codes_in[:].rearrange("p (m t) -> p m t", t=PACK)[:, :, 2 * u : 2 * u + 2],
+            )
+            w_pairs.append(w_pair)
+        w_codes = [w_pairs[t // 2][:, t % 2, :].bitcast(E5M2) for t in range(PACK)]
+        w_plane = sb.tile([P, PACK, P], U8, name="w_plane", align_bytes=64)
+        nc.vector.tensor_copy(out=w_plane[:], in_=w_plane_in[:].rearrange("p (m t) -> p t m", t=PACK))
+
+        nc.vector.tensor_copy(out=x2_plane[:], in_=xt_plane[:].indirect(second_list[:]))
+        x2_codes = sb.tile([P, J], U16, name="x2_codes", tag="w_plane_in", align_bytes=64)
+        nc.vector.tensor_copy(out=x2_codes[:], in_=xt_codes[:].indirect(second_list[:]))
+
+        late_codes = sb.tile([P, 2 * N], U32, name="late_codes", tag="w_codes_in", align_bytes=64)
+        ws_codes, wb_codes = late_codes[:, 0:N], late_codes[:, N : 2 * N]
+        load_words(nc, ws_codes, ws_words[0].rearrange("p n t -> p (n t)"))
+        load_words(nc, wb_codes, wb_words[0].rearrange("p n t -> p (n t)"))
+
+        a_all = stage.tile([P, PACK, J], F32, name="a_all", offset=0)
+        a_sb = [a_all[:, t, :] for t in range(PACK)]
+        for t in range(PACK):
+            a_bank = psum.tile([P, J], F32, name=f"a_bank{t}", tag=f"bank{t}")
+            nc.tensor.matmul_mx(
+                out=a_bank[:], lhsT=w_codes[t], lhsT_scale=w_plane[:, t, :],
+                rhs=x1_codes[:].bitcast(E2M1), rhs_scale=x1_plane[:], start=True, stop=True,
+            )
+            nc.scalar.activation(out=a_sb[t], in_=a_bank[:], func=COPY)
+
+        b_banks = []
+        for h in range(2):
+            cols = slice(h * HALF, (h + 1) * HALF)
+            b_bank = psum.tile([P, PACK, HALF], F32, name=f"b_bank{h}")
+            for t in range(PACK):
+                nc.tensor.matmul_mx(
+                    out=b_bank[:, t, :], lhsT=w_codes[t], lhsT_scale=w_plane[:, t, :],
+                    rhs=x2_codes[:, cols].bitcast(E2M1), rhs_scale=x2_plane[:, cols], start=True, stop=True,
+                )
+            b_banks.append(b_bank)
+
+        p_first = psum.tile([P, 2, HALF], F32, name="p_first")
+        p_second = [psum.tile([P, HALF], F32, name=f"p_second{n}", tag=f"bank{n}") for n in range(2)]
+
+        def p_pass(h, n, codes, plane, rhs, rhs_plane, last):
+            rows = slice(n * P, (n + 1) * P)
+            if h == 0:
+                sums, start, stop = p_first[:, n, :], (n == 0 and not last), (n == 1 and last)
+            else:
+                sums, start, stop = p_second[n][:], not last, last
+            nc.tensor.matmul_mx(
+                out=sums, lhsT=codes[:, rows].bitcast(E4M3), lhsT_scale=plane[:, rows],
+                rhs=rhs, rhs_scale=rhs_plane, start=start, stop=stop,
+            )
+
+        for h in range(2):
+            cols = slice(h * HALF, (h + 1) * HALF)
+            for n in range(2):
+                p_pass(h, n, ws_codes, ws_plane, x1_codes[:, cols].bitcast(E2M1), x1_plane[:, cols], False)
+
+        pages = [
+            sb.tile([P, E], F32, name="page0", tag="xt_codes", align_bytes=64),
+            sb.tile([P, E], F32, name="page1", tag="xt_plane", align_bytes=64),
+        ]
+        for n in range(2):
+            nc.gpsimd.memset(pages[n][:], 0.0)
+
+        def put(t, first, last, on_scalar):
+            entries = put_list[:, first // 16 : last // 16]
+            move(nc, on_scalar, boards[t][:].indirect(entries), a_sb[t][:, first:last])
+
+        put(0, 0, J, False)
+        put(1, 0, J, False)
+        put(2, 0, SPLIT, True)
+        put(3, 0, J, True)
+        put(2, SPLIT, J, False)
+
+        picked = [stage.tile([P, PACK, HALF], F32, name=f"picked{h}", offset=h * PACK * HALF * 4) for h in range(2)]
+
+        def pick(h, t, on_scalar):
+            entries = read_list[:, h * HALF_COLS : (h + 1) * HALF_COLS]
+            move(nc, on_scalar, picked[h][:, t, :], boards[t][:].indirect(entries))
+
+        def larger(h):
+            hid = sb.tile([P, HALF * PACK], BF16, name=f"hid{h}", tag="hid", align_bytes=64)
+            nc.vector.tensor_tensor(
+                out=hid[:].rearrange("p (c i t) -> p c t i", i=4, t=PACK),
+                in0=picked[h][:].rearrange("p t (c i) -> p c t i", i=4),
+                in1=b_banks[h][:].rearrange("p t (c i) -> p c t i", i=4),
+                op=MAX,
+            )
+            return hid
+
+        def quantize_and_multiply(h, hid):
+            hid_codes = sb.tile([P, HALF], U32, name=f"hid_codes{h}", align_bytes=64)
+            hid_plane = sb.tile([P, HALF], U8, name=f"hid_plane{h}", align_bytes=64)
+            nc.vector.quantize_mx(out=hid_codes[:].bitcast(E5M2), scales=hid_plane[:], in_=hid[:])
+            for n in range(2):
+                p_pass(h, n, wb_codes, wb_plane, hid_codes[:].bitcast(E5M2), hid_plane[:], True)
+
+        def put_out(h, n, values):
+            entries = page_list[:, h * HALF_COLS : (h + 1) * HALF_COLS]
+            move(nc, n == 0, pages[n][:].indirect(entries), values)
+
+        pick(0, 0, False)
+        pick(0, 1, False)
+        pick(0, 2, False)
+        pick(0, 3, True)
+        hid0 = larger(0)
+        pick(1, 0, True)
+        pick(1, 1, True)
+        pick(1, 2, True)
+        pick(1, 3, True)
+        quantize_and_multiply(0, hid0)
+        hid1 = larger(1)
+        p_sb0 = sb.tile([P, 2, HALF], F32, name="p_sb0")
+        move(nc, True, p_sb0[:], p_first[:])
+        quantize_and_multiply(1, hid1)
+        for n in range(2):
+            put_out(0, n, p_sb0[:, n, :])
+        for n in range(2):
+            p_sb1 = sb.tile([P, HALF], F32, name=f"p_sb1{n}")
+            move(nc, n == 0, p_sb1[:], p_second[n][:])
+            put_out(1, n, p_sb1[:])
+        for n in range(2):
+            nc.sync.dma_start(out=out[n * P : (n + 1) * P, :], in_=pages[n][:])

@@ -21,7 +21,6 @@ P = 128
 PACK = 4
 HALF = J // 2
 HALF_COLS = HALF // 16
-SPLIT = 192
 
 
 def load_words(nc, tile, words):
@@ -29,11 +28,8 @@ def load_words(nc, tile, words):
 
 
 def load_scale_rows(queue, plane, scales):
-    for q in range(4):
-        queue.dma_start(
-            out=plane[32 * q : 32 * q + 4, :].bitcast(I32),
-            in_=scales[0, 4 * q : 4 * q + 4, :].bitcast(I32),
-        )
+    for r in range(4):
+        queue.dma_start(out=plane[r:P:32, :].bitcast(I32), in_=scales[0, r:16:4, :].bitcast(I32))
 
 
 def move(nc, on_scalar, out, in_):
@@ -63,13 +59,14 @@ def tile_list_tied_board_skip_scattered_kernel(
         xt_codes = sb.tile([P, T], U16, name="xt_codes", tag="xt_codes", align_bytes=64)
         xt_plane = sb.tile([P, T], U8, name="xt_plane", tag="xt_plane", align_bytes=64)
         w_codes_in = sb.tile([P, R], U32, name="w_codes_in", tag="w_codes_in", align_bytes=64)
-        w_plane_in = sb.tile([P, R], U8, name="w_plane_in", tag="w_plane_in", align_bytes=64)
+        w_plane_in = stage.tile([P, R], U8, name="w_plane_in", align_bytes=64, offset=192)
+        pages = [sb.tile([P, E], F32, name=f"page{n}") for n in range(2)]
         ws_plane = sb.tile([P, N], U8, name="ws_plane", align_bytes=64)
         wb_plane = sb.tile([P, N], U8, name="wb_plane", align_bytes=64)
         boards = [sb.tile([P, C], F32, name=f"board{t}") for t in range(PACK)]
 
         nc.vector.memset(xt_plane[:].bitcast(I32), 0)
-        nc.gpsimd.memset(w_plane_in[:].bitcast(I32), 0)
+        nc.vector.memset(w_plane_in[:].bitcast(I32), 0)
 
         nc.sync.dma_start(first_list[:], offs)
         nc.sync.dma_start(second_list[:], offs2)
@@ -80,9 +77,11 @@ def tile_list_tied_board_skip_scattered_kernel(
         load_scale_rows(nc.sync, w_plane_in, w_scales)
 
         for t in range(PACK):
-            nc.gpsimd.memset(boards[t][:], 0.0)
+            nc.vector.memset(boards[t][:].bitcast(I32), 0)
         nc.vector.memset(ws_plane[:].bitcast(I32), 0)
         nc.vector.memset(wb_plane[:].bitcast(I32), 0)
+        for n in range(2):
+            nc.vector.memset(pages[n][:].bitcast(I32), 0)
 
         nc.sync.dma_start(read_list[:], offs4)
         nc.sync.dma_start(page_list[:], offs5)
@@ -91,7 +90,6 @@ def tile_list_tied_board_skip_scattered_kernel(
 
         x1_plane = sb.tile([P, J], U8, name="x1_plane", align_bytes=64)
         x1_codes = sb.tile([P, J], U16, name="x1_codes", align_bytes=64)
-        x2_plane = sb.tile([P, J], U8, name="x2_plane", align_bytes=64)
         nc.vector.tensor_copy(out=x1_plane[:], in_=xt_plane[:].indirect(first_list[:]))
         nc.vector.tensor_copy(out=x1_codes[:], in_=xt_codes[:].indirect(first_list[:]))
 
@@ -104,11 +102,19 @@ def tile_list_tied_board_skip_scattered_kernel(
             )
             w_pairs.append(w_pair)
         w_codes = [w_pairs[t // 2][:, t % 2, :].bitcast(E5M2) for t in range(PACK)]
-        w_plane = sb.tile([P, PACK, P], U8, name="w_plane", align_bytes=64)
-        nc.vector.tensor_copy(out=w_plane[:], in_=w_plane_in[:].rearrange("p (m t) -> p t m", t=PACK))
+        w_plane_pairs = []
+        for u in range(2):
+            w_plane_pair = sb.tile([P, 2, P], U8, name=f"w_plane_pair{u}", align_bytes=64)
+            nc.vector.tensor_copy(
+                out=w_plane_pair[:],
+                in_=w_plane_in[:].rearrange("p (m t) -> p t m", t=PACK)[:, 2 * u : 2 * u + 2, :],
+            )
+            w_plane_pairs.append(w_plane_pair)
+        w_planes = [w_plane_pairs[t // 2][:, t % 2, :] for t in range(PACK)]
 
+        x2_plane = stage.tile([P, J], U8, name="x2_plane", align_bytes=64, offset=0)
         nc.vector.tensor_copy(out=x2_plane[:], in_=xt_plane[:].indirect(second_list[:]))
-        x2_codes = sb.tile([P, J], U16, name="x2_codes", tag="w_plane_in", align_bytes=64)
+        x2_codes = stage.tile([P, J], U16, name="x2_codes", align_bytes=64, offset=256)
         nc.vector.tensor_copy(out=x2_codes[:], in_=xt_codes[:].indirect(second_list[:]))
 
         late_codes = sb.tile([P, 2 * N], U32, name="late_codes", tag="w_codes_in", align_bytes=64)
@@ -116,15 +122,14 @@ def tile_list_tied_board_skip_scattered_kernel(
         load_words(nc, ws_codes, ws_words[0].rearrange("p n t -> p (n t)"))
         load_words(nc, wb_codes, wb_words[0].rearrange("p n t -> p (n t)"))
 
-        a_all = stage.tile([P, PACK, J], F32, name="a_all", offset=0)
-        a_sb = [a_all[:, t, :] for t in range(PACK)]
+        a_sb = [sb.tile([P, J], F32, name=f"a_sb{t}") for t in range(PACK)]
         for t in range(PACK):
             a_bank = psum.tile([P, J], F32, name=f"a_bank{t}", tag=f"bank{t}")
             nc.tensor.matmul_mx(
-                out=a_bank[:], lhsT=w_codes[t], lhsT_scale=w_plane[:, t, :],
+                out=a_bank[:], lhsT=w_codes[t], lhsT_scale=w_planes[t],
                 rhs=x1_codes[:].bitcast(E2M1), rhs_scale=x1_plane[:], start=True, stop=True,
             )
-            nc.scalar.activation(out=a_sb[t], in_=a_bank[:], func=COPY)
+            nc.scalar.activation(out=a_sb[t][:], in_=a_bank[:], func=COPY)
 
         b_banks = []
         for h in range(2):
@@ -132,93 +137,60 @@ def tile_list_tied_board_skip_scattered_kernel(
             b_bank = psum.tile([P, PACK, HALF], F32, name=f"b_bank{h}")
             for t in range(PACK):
                 nc.tensor.matmul_mx(
-                    out=b_bank[:, t, :], lhsT=w_codes[t], lhsT_scale=w_plane[:, t, :],
+                    out=b_bank[:, t, :], lhsT=w_codes[t], lhsT_scale=w_planes[t],
                     rhs=x2_codes[:, cols].bitcast(E2M1), rhs_scale=x2_plane[:, cols], start=True, stop=True,
                 )
             b_banks.append(b_bank)
 
-        p_first = psum.tile([P, 2, HALF], F32, name="p_first")
-        p_second = [psum.tile([P, HALF], F32, name=f"p_second{n}", tag=f"bank{n}") for n in range(2)]
-
-        def p_pass(h, n, codes, plane, rhs, rhs_plane, last):
-            rows = slice(n * P, (n + 1) * P)
-            if h == 0:
-                sums, start, stop = p_first[:, n, :], (n == 0 and not last), (n == 1 and last)
-            else:
-                sums, start, stop = p_second[n][:], not last, last
-            nc.tensor.matmul_mx(
-                out=sums, lhsT=codes[:, rows].bitcast(E4M3), lhsT_scale=plane[:, rows],
-                rhs=rhs, rhs_scale=rhs_plane, start=start, stop=stop,
-            )
-
+        p_banks = {}
         for h in range(2):
             cols = slice(h * HALF, (h + 1) * HALF)
             for n in range(2):
-                p_pass(h, n, ws_codes, ws_plane, x1_codes[:, cols].bitcast(E2M1), x1_plane[:, cols], False)
+                rows = slice(n * P, (n + 1) * P)
+                p_bank = psum.tile([P, HALF], F32, name=f"p_bank{h}{n}", tag=f"bank{2 * h + n}")
+                nc.tensor.matmul_mx(
+                    out=p_bank[:], lhsT=ws_codes[:, rows].bitcast(E4M3), lhsT_scale=ws_plane[:, rows],
+                    rhs=x1_codes[:, cols].bitcast(E2M1), rhs_scale=x1_plane[:, cols], start=True, stop=False,
+                )
+                p_banks[h, n] = p_bank
 
-        pages = [
-            sb.tile([P, E], F32, name="page0", tag="xt_codes", align_bytes=64),
-            sb.tile([P, E], F32, name="page1", tag="xt_plane", align_bytes=64),
-        ]
-        for n in range(2):
-            nc.gpsimd.memset(pages[n][:], 0.0)
+        for t in range(PACK):
+            move(nc, t >= 2, boards[t][:].indirect(put_list[:]), a_sb[t][:])
 
-        def put(t, first, last, on_scalar):
-            entries = put_list[:, first // 16 : last // 16]
-            move(nc, on_scalar, boards[t][:].indirect(entries), a_sb[t][:, first:last])
-
-        put(0, 0, J, False)
-        put(1, 0, J, False)
-        put(2, 0, SPLIT, True)
-        put(3, 0, J, True)
-        put(2, SPLIT, J, False)
-
-        picked = [stage.tile([P, PACK, HALF], F32, name=f"picked{h}", offset=h * PACK * HALF * 4) for h in range(2)]
-
-        def pick(h, t, on_scalar):
+        hids = []
+        for h in range(2):
+            picked = sb.tile([P, PACK, HALF], F32, name=f"picked{h}")
             entries = read_list[:, h * HALF_COLS : (h + 1) * HALF_COLS]
-            move(nc, on_scalar, picked[h][:, t, :], boards[t][:].indirect(entries))
-
-        def larger(h):
-            hid = sb.tile([P, HALF * PACK], BF16, name=f"hid{h}", tag="hid", align_bytes=64)
+            for t in range(PACK):
+                move(nc, t >= 2, picked[:, t, :], boards[t][:].indirect(entries))
+            hid = sb.tile([P, HALF * PACK], BF16, name=f"hid{h}", align_bytes=64)
             nc.vector.tensor_tensor(
                 out=hid[:].rearrange("p (c i t) -> p c t i", i=4, t=PACK),
-                in0=picked[h][:].rearrange("p t (c i) -> p c t i", i=4),
+                in0=picked[:].rearrange("p t (c i) -> p c t i", i=4),
                 in1=b_banks[h][:].rearrange("p t (c i) -> p c t i", i=4),
                 op=MAX,
             )
-            return hid
+            hids.append(hid)
 
-        def quantize_and_multiply(h, hid):
+        for h in range(2):
             hid_codes = sb.tile([P, HALF], U32, name=f"hid_codes{h}", align_bytes=64)
             hid_plane = sb.tile([P, HALF], U8, name=f"hid_plane{h}", align_bytes=64)
-            nc.vector.quantize_mx(out=hid_codes[:].bitcast(E5M2), scales=hid_plane[:], in_=hid[:])
+            nc.vector.quantize_mx(out=hid_codes[:].bitcast(E5M2), scales=hid_plane[:], in_=hids[h][:])
             for n in range(2):
-                p_pass(h, n, wb_codes, wb_plane, hid_codes[:].bitcast(E5M2), hid_plane[:], True)
+                rows = slice(n * P, (n + 1) * P)
+                nc.tensor.matmul_mx(
+                    out=p_banks[h, n][:], lhsT=wb_codes[:, rows].bitcast(E4M3), lhsT_scale=wb_plane[:, rows],
+                    rhs=hid_codes[:].bitcast(E5M2), rhs_scale=hid_plane[:], start=False, stop=True,
+                )
 
-        def put_out(h, n, values):
+        p_sb = {}
+        for h in range(2):
+            for n in range(2):
+                p_sb[h, n] = sb.tile([P, HALF], F32, name=f"p_sb{h}{n}")
+                move(nc, n == 0, p_sb[h, n][:], p_banks[h, n][:])
+        for h in range(2):
             entries = page_list[:, h * HALF_COLS : (h + 1) * HALF_COLS]
-            move(nc, n == 0, pages[n][:].indirect(entries), values)
-
-        pick(0, 0, False)
-        pick(0, 1, False)
-        pick(0, 2, False)
-        pick(0, 3, True)
-        hid0 = larger(0)
-        pick(1, 0, True)
-        pick(1, 1, True)
-        pick(1, 2, True)
-        pick(1, 3, True)
-        quantize_and_multiply(0, hid0)
-        hid1 = larger(1)
-        p_sb0 = sb.tile([P, 2, HALF], F32, name="p_sb0")
-        move(nc, True, p_sb0[:], p_first[:])
-        quantize_and_multiply(1, hid1)
-        for n in range(2):
-            put_out(0, n, p_sb0[:, n, :])
-        for n in range(2):
-            p_sb1 = sb.tile([P, HALF], F32, name=f"p_sb1{n}")
-            move(nc, n == 0, p_sb1[:], p_second[n][:])
-            put_out(1, n, p_sb1[:])
+            for n in range(2):
+                move(nc, n == 0, pages[n][:].indirect(entries), p_sb[h, n][:])
         for n in range(2):
             nc.sync.dma_start(out=out[n * P : (n + 1) * P, :], in_=pages[n][:])

@@ -73,8 +73,8 @@ def tile_list_tied_board_skip_scattered_kernel(
         nc.sync.dma_start(put_list[:], offs3)
         load_scale_rows(nc.sync, xt_plane, xt_scales)
         load_words(nc, xt_codes, xt_words[0])
-        load_words(nc, w_codes_in, w_words[0].rearrange("p n t -> p (n t)"))
         load_scale_rows(nc.sync, w_plane_in, w_scales)
+        load_words(nc, w_codes_in, w_words[0].rearrange("p n t -> p (n t)"))
 
         for t in range(PACK):
             nc.vector.memset(boards[t][:].bitcast(I32), 0)

@@ -61,8 +61,8 @@ def tile_list_tied_board_skip_scattered_kernel(
         w_codes_in = sb.tile([P, R], U32, name="w_codes_in", tag="w_codes_in", align_bytes=64)
         w_plane_in = stage.tile([P, R], U8, name="w_plane_in", align_bytes=64, offset=192)
         pages = [sb.tile([P, E], F32, name=f"page{n}") for n in range(2)]
-        ws_plane = sb.tile([P, N], U8, name="ws_plane", align_bytes=64)
-        wb_plane = sb.tile([P, N], U8, name="wb_plane", align_bytes=64)
+        late_planes = sb.tile([P, 2 * N], U8, name="late_planes", align_bytes=64)
+        ws_plane, wb_plane = late_planes[:, 0:N], late_planes[:, N : 2 * N]
         boards = [sb.tile([P, C], F32, name=f"board{t}") for t in range(PACK)]
 
         nc.vector.memset(xt_plane[:].bitcast(I32), 0)
@@ -78,8 +78,7 @@ def tile_list_tied_board_skip_scattered_kernel(
 
         for t in range(PACK):
             nc.vector.memset(boards[t][:].bitcast(I32), 0)
-        nc.vector.memset(ws_plane[:].bitcast(I32), 0)
-        nc.vector.memset(wb_plane[:].bitcast(I32), 0)
+        nc.vector.memset(late_planes[:].bitcast(I32), 0)
         for n in range(2):
             nc.vector.memset(pages[n][:].bitcast(I32), 0)
 
@@ -165,9 +164,9 @@ def tile_list_tied_board_skip_scattered_kernel(
                 move(nc, t >= 2, picked[:, t, :], boards[t][:].indirect(entries))
             hid = sb.tile([P, HALF * PACK], BF16, name=f"hid{h}", align_bytes=64)
             nc.vector.tensor_tensor(
-                out=hid[:].rearrange("p (c i t) -> p c t i", i=4, t=PACK),
-                in0=picked[:].rearrange("p t (c i) -> p c t i", i=4),
-                in1=b_banks[h][:].rearrange("p t (c i) -> p c t i", i=4),
+                out=hid[:].rearrange("p (c i t) -> p c t i", i=2, t=PACK),
+                in0=picked[:].rearrange("p t (c i) -> p c t i", i=2),
+                in1=b_banks[h][:].rearrange("p t (c i) -> p c t i", i=2),
                 op=MAX,
             )
             hids.append(hid)

from contextlib import ExitStack

import concourse.mybir as mybir

K, T, J, R, C, N, E = 512, 2048, 256, 512, 512, 256, 1024
FLOPS = 2 * K * R * J * 2 + 2 * R * N * J + 2 * K * N * J

F32 = mybir.dt.float32
BF16 = mybir.dt.bfloat16
I32 = mybir.dt.int32
U32 = mybir.dt.uint32
U16 = mybir.dt.uint16
U8 = mybir.dt.uint8
E4M3 = mybir.dt.float8_e4m3fn_x4
E5M2 = mybir.dt.float8_e5m2_x4
E2M1 = mybir.dt.float4_e2m1fn_x4
COPY = mybir.ActivationFunctionType.Copy
MAX = mybir.AluOpType.max

P = 128
PACK = 4
HALF = J // 2
HALF_COLS = HALF // 16


def load_words(nc, tile, words):
    nc.sync.dma_start(out=tile[:].bitcast(I32), in_=words.bitcast(I32))


def load_scale_rows(queue, plane, scales):
    for r in range(4):
        queue.dma_start(out=plane[r:P:32, :].bitcast(I32), in_=scales[0, r:16:4, :].bitcast(I32))


def move(nc, on_scalar, out, in_):
    if on_scalar:
        nc.scalar.activation(out=out, in_=in_, func=COPY)
    else:
        nc.vector.tensor_copy(out=out, in_=in_)


def tile_list_tied_board_skip_scattered_kernel(
    tc, xt_words, xt_scales, w_words, w_scales, wb_words, wb_scales, ws_words, ws_scales,
    offs, offs2, offs3, offs4, offs5, out,
):
    nc = tc.nc
    with ExitStack() as ctx:
        lists = ctx.enter_context(tc.tile_pool(name="lists", bufs=1))
        sb = ctx.enter_context(tc.tile_pool(name="sb", bufs=1))
        stage = ctx.enter_context(tc.tile_pool(name="stage", bufs=1))
        psum = ctx.enter_context(tc.psum_pool(name="psum", bufs=1))

        first_list = lists.tile([P, J // 16], U16, name="first_list")
        second_list = lists.tile([P, J // 16], U16, name="second_list")
        put_list = lists.tile([P, J // 16], U16, name="put_list")
        read_list = lists.tile([P, J // 16], U16, name="read_list")
        page_list = lists.tile([P, J // 16], U16, name="page_list")

        xt_codes = sb.tile([P, T], U16, name="xt_codes", tag="xt_codes", align_bytes=64)
        xt_plane = sb.tile([P, T], U8, name="xt_plane", tag="xt_plane", align_bytes=64)
        w_codes_in = sb.tile([P, R], U32, name="w_codes_in", tag="w_codes_in", align_bytes=64)
        w_plane_in = stage.tile([P, R], U8, name="w_plane_in", align_bytes=64, offset=192)
        pages = [sb.tile([P, E], F32, name=f"page{n}") for n in range(2)]
        late_planes = sb.tile([P, 2 * N], U8, name="late_planes", align_bytes=64)
        ws_plane, wb_plane = late_planes[:, 0:N], late_planes[:, N : 2 * N]
        boards = [sb.tile([P, C], F32, name=f"board{t}") for t in range(PACK)]

        nc.vector.memset(xt_plane[:].bitcast(I32), 0)
        nc.vector.memset(w_plane_in[:].bitcast(I32), 0)

        nc.sync.dma_start(first_list[:], offs)
        nc.sync.dma_start(second_list[:], offs2)
        nc.sync.dma_start(put_list[:], offs3)
        load_scale_rows(nc.sync, xt_plane, xt_scales)
        load_words(nc, xt_codes, xt_words[0])
        load_scale_rows(nc.sync, w_plane_in, w_scales)
        load_words(nc, w_codes_in, w_words[0].rearrange("p n t -> p (n t)"))

        for t in range(PACK):
            nc.vector.memset(boards[t][:].bitcast(I32), 0)
        nc.vector.memset(late_planes[:].bitcast(I32), 0)
        for n in range(2):
            nc.vector.memset(pages[n][:].bitcast(I32), 0)

        nc.sync.dma_start(read_list[:], offs4)
        nc.sync.dma_start(page_list[:], offs5)
        load_scale_rows(nc.sync, ws_plane, ws_scales)
        load_scale_rows(nc.sync, wb_plane, wb_scales)

        x1_plane = sb.tile([P, J], U8, name="x1_plane", align_bytes=64)
        x1_codes = sb.tile([P, J], U16, name="x1_codes", align_bytes=64)
        nc.vector.tensor_copy(out=x1_plane[:], in_=xt_plane[:].indirect(first_list[:]))
        nc.vector.tensor_copy(out=x1_codes[:], in_=xt_codes[:].indirect(first_list[:]))

        w_pairs = []
        for u in range(2):
            w_pair = sb.tile([P, 2, P], U32, name=f"w_pair{u}", align_bytes=64)
            nc.scalar.copy(
                out=w_pair[:].rearrange("p t m -> p m t"),
                in_=w_codes_in[:].rearrange("p (m t) -> p m t", t=PACK)[:, :, 2 * u : 2 * u + 2],
            )
            w_pairs.append(w_pair)
        w_codes = [w_pairs[t // 2][:, t % 2, :].bitcast(E5M2) for t in range(PACK)]
        w_plane_pairs = []
        for u in range(2):
            w_plane_pair = sb.tile([P, 2, P], U8, name=f"w_plane_pair{u}", align_bytes=64)
            nc.vector.tensor_copy(
                out=w_plane_pair[:],
                in_=w_plane_in[:].rearrange("p (m t) -> p t m", t=PACK)[:, 2 * u : 2 * u + 2, :],
            )
            w_plane_pairs.append(w_plane_pair)
        w_planes = [w_plane_pairs[t // 2][:, t % 2, :] for t in range(PACK)]

        x2_plane = stage.tile([P, J], U8, name="x2_plane", align_bytes=64, offset=0)
        nc.vector.tensor_copy(out=x2_plane[:], in_=xt_plane[:].indirect(second_list[:]))
        x2_codes = stage.tile([P, J], U16, name="x2_codes", align_bytes=64, offset=256)
        nc.vector.tensor_copy(out=x2_codes[:], in_=xt_codes[:].indirect(second_list[:]))

        late_codes = sb.tile([P, 2 * N], U32, name="late_codes", tag="w_codes_in", align_bytes=64)
        ws_codes, wb_codes = late_codes[:, 0:N], late_codes[:, N : 2 * N]
        load_words(nc, ws_codes, ws_words[0].rearrange("p n t -> p (n t)"))
        load_words(nc, wb_codes, wb_words[0].rearrange("p n t -> p (n t)"))

        a_sb = [sb.tile([P, J], F32, name=f"a_sb{t}") for t in range(PACK)]
        for t in range(PACK):
            a_bank = psum.tile([P, J], F32, name=f"a_bank{t}", tag=f"bank{t}")
            nc.tensor.matmul_mx(
                out=a_bank[:], lhsT=w_codes[t], lhsT_scale=w_planes[t],
                rhs=x1_codes[:].bitcast(E2M1), rhs_scale=x1_plane[:], start=True, stop=True,
            )
            nc.scalar.activation(out=a_sb[t][:], in_=a_bank[:], func=COPY)

        b_banks = []
        for h in range(2):
            cols = slice(h * HALF, (h + 1) * HALF)
            b_bank = psum.tile([P, PACK, HALF], F32, name=f"b_bank{h}")
            for t in range(PACK):
                nc.tensor.matmul_mx(
                    out=b_bank[:, t, :], lhsT=w_codes[t], lhsT_scale=w_planes[t],
                    rhs=x2_codes[:, cols].bitcast(E2M1), rhs_scale=x2_plane[:, cols], start=True, stop=True,
                )
            b_banks.append(b_bank)

        p_banks = {}
        for h in range(2):
            cols = slice(h * HALF, (h + 1) * HALF)
            for n in range(2):
                rows = slice(n * P, (n + 1) * P)
                p_bank = psum.tile([P, HALF], F32, name=f"p_bank{h}{n}", tag=f"bank{2 * h + n}")
                nc.tensor.matmul_mx(
                    out=p_bank[:], lhsT=ws_codes[:, rows].bitcast(E4M3), lhsT_scale=ws_plane[:, rows],
                    rhs=x1_codes[:, cols].bitcast(E2M1), rhs_scale=x1_plane[:, cols], start=True, stop=False,
                )
                p_banks[h, n] = p_bank

        for t in range(PACK):
            move(nc, t >= 2, boards[t][:].indirect(put_list[:]), a_sb[t][:])

        hids = []
        for h in range(2):
            picked = sb.tile([P, PACK, HALF], F32, name=f"picked{h}")
            entries = read_list[:, h * HALF_COLS : (h + 1) * HALF_COLS]
            for t in range(PACK):
                move(nc, t >= 2, picked[:, t, :], boards[t][:].indirect(entries))
            hid = sb.tile([P, HALF * PACK], BF16, name=f"hid{h}", align_bytes=64)
            nc.vector.tensor_tensor(
                out=hid[:].rearrange("p (c i t) -> p c t i", i=2, t=PACK),
                in0=picked[:].rearrange("p t (c i) -> p c t i", i=2),
                in1=b_banks[h][:].rearrange("p t (c i) -> p c t i", i=2),
                op=MAX,
            )
            hids.append(hid)

        for h in range(2):
            hid_codes = sb.tile([P, HALF], U32, name=f"hid_codes{h}", align_bytes=64)
            hid_plane = sb.tile([P, HALF], U8, name=f"hid_plane{h}", align_bytes=64)
            nc.vector.quantize_mx(out=hid_codes[:].bitcast(E5M2), scales=hid_plane[:], in_=hids[h][:])
            for n in range(2):
                rows = slice(n * P, (n + 1) * P)
                nc.tensor.matmul_mx(
                    out=p_banks[h, n][:], lhsT=wb_codes[:, rows].bitcast(E4M3), lhsT_scale=wb_plane[:, rows],
                    rhs=hid_codes[:].bitcast(E5M2), rhs_scale=hid_plane[:], start=False, stop=True,
                )

        p_sb = {}
        for h in range(2):
            for n in range(2):
                p_sb[h, n] = sb.tile([P, HALF], F32, name=f"p_sb{h}{n}")
                move(nc, n == 0, p_sb[h, n][:], p_banks[h, n][:])
        for h in range(2):
            entries = page_list[:, h * HALF_COLS : (h + 1) * HALF_COLS]
            for n in range(2):
                move(nc, n == 0, pages[n][:].indirect(entries), p_sb[h, n][:])
        for n in range(2):
            nc.sync.dma_start(out=out[n * P : (n + 1) * P, :], in_=pages[n][:])
